import numpy as np
import ml_dtypes


def mxq(x, axis, fmt="e4m3"):
    dtype, down = {"e4m3": (ml_dtypes.float8_e4m3fn, 7), "e5m2": (ml_dtypes.float8_e5m2, 14)}[fmt]
    v = np.moveaxis(np.asarray(x, np.float32).astype(ml_dtypes.bfloat16).astype(np.float64), axis, -1)
    blocks = v.reshape(v.shape[:-1] + (-1, 32))
    amax = np.abs(blocks).max(-1, keepdims=True)
    byte = np.maximum(np.where(amax > 0, np.frexp(amax)[1] - 1 + 127, 0) - down, 1)
    scale = np.exp2(byte - 127.0)
    codes = (blocks / scale).astype(np.float32).astype(dtype).astype(np.float64)
    return np.moveaxis((codes * scale).reshape(v.shape), -1, axis)


WIDE = False


def mx_kscale(k):
    if not WIDE:
        return np.ones(k)
    levels = np.array([10, -10, 5, -5, 0])
    if k % 512:
        return np.exp2(np.random.permutation(np.resize(levels, k // 32))).repeat(32)
    a = np.empty((k // 512, 16))
    for p in range(k // 512):
        a[p, :8] = np.random.permutation(np.resize(levels, 8))
        for g in range(8):
            far = levels[np.abs(levels - a[p, g]) >= 10]
            a[p, g + 8] = far[np.random.randint(len(far))]
    return np.exp2(a.ravel()).repeat(32)


def f64(x):
    return np.asarray(x).astype(np.float64)


def striped(idx):
    return np.tile(np.asarray(idx).reshape(-1, 16).T, (8, 1)).astype(np.uint16)


def unstriped(offs):
    return offs[:16].T.reshape(-1).astype(np.int64)


E2M1 = np.array([0.0, 0.5, 1.0, 1.5, 2.0, 3.0, 4.0, 6.0, -0.0, -0.5, -1.0, -1.5, -2.0, -3.0, -4.0, -6.0])


def pack_weight(w, fmt):
    k, n = w.shape
    w = f64(np.asarray(w, np.float32).astype(ml_dtypes.bfloat16)).reshape(k // 32, 32, n)
    amax = np.abs(w).max(1)
    if fmt == "e4m3":
        byte = np.frexp(amax)[1] - 1 + 127 - 7
    else:
        mant, ex = np.frexp(amax / 6.0)
        byte = np.where(mant > 0.5, ex, ex - 1) + 127
    byte = np.clip(np.where(amax > 0, byte, 1), 1, 254)
    scaled = (w * np.exp2(127.0 - byte)[:, None, :]).reshape(k, n).astype(np.float32)
    by_word = np.ascontiguousarray(scaled.reshape(k // 512, 128, 4, n).transpose(0, 1, 3, 2))
    if fmt == "e4m3":
        words = by_word.astype(ml_dtypes.float8_e4m3fn).view(np.uint8)
    else:
        c = by_word.astype(ml_dtypes.float4_e2m1fn).view(np.uint8) & 0xF
        words = (c[..., 0::2] | (c[..., 1::2] << 4)).reshape(k // 512, 128, 2 * n)
    return np.ascontiguousarray(words), np.ascontiguousarray(byte.astype(np.uint8).reshape(k // 512, 16, n))


def unpack_weight(words, scales, fmt):
    g, _, n = scales.shape
    words = np.ascontiguousarray(words).reshape(g, 128, n, -1)
    if fmt == "e4m3":
        vals = words.view(ml_dtypes.float8_e4m3fn).astype(np.float64)
    else:
        nib = np.empty((g, 128, n, 4), np.uint8)
        nib[..., 0::2] = words & 0xF
        nib[..., 1::2] = words >> 4
        vals = E2M1[nib]
    vals = vals * np.repeat(np.exp2(scales.astype(np.float64) - 127.0), 8, axis=1)[..., None]
    return vals.transpose(0, 1, 3, 2).reshape(g * 512, n)


def bf(x):
    return np.asarray(x, np.float32).astype(ml_dtypes.bfloat16)


def planes(Y):
    r, m = Y.shape
    b = f64(bf(Y)).reshape(r // 32, 32, m)
    amax = np.abs(b).max(1)
    byte = np.clip(np.where(amax > 0, np.frexp(amax)[1] - 1 + 127 - 7, 1), 1, 254)
    codes = (b * np.exp2(127.0 - byte)[:, None, :]).reshape(r, m).astype(np.float32).astype(ml_dtypes.float8_e4m3fn).view(np.uint8)
    words = codes.reshape(r // 512, 128, 4, m).transpose(0, 1, 3, 2)
    return np.ascontiguousarray(words), np.ascontiguousarray(byte.astype(np.uint8).reshape(r // 512, 16, m))


D, T, I, Q, E, K = 512, 1024, 512, 256, 512, 1024


def setup_inputs():
    n = np.random.standard_normal
    idx = np.random.permutation(T)[:I]
    fd = mx_kscale(D)
    fk = mx_kscale(K)
    fi = mx_kscale(I)
    ti = np.ones(T)
    ti[idx] = fi
    krestp = pack_weight(n((K, T)) / fk[:, None], "e2m1")
    return {
        "query": (n((D, Q)) * 0.3 / np.sqrt(D) * fd[:, None]).astype(np.float32),
        "kfirst": (n((D, T)) / fd[:, None]).astype(np.float32),
        "qrest": (n((K, Q)) * 0.45 / np.sqrt(K) * fk[:, None]).astype(np.float32),
        "krest_words": krestp[0],
        "krest_scales": krestp[1],
        "size": (np.random.uniform(0.5, 2.0, (1, I)) * fi).astype(np.float32),
        "vals": (n((E, T)) / ti).astype(np.float32),
        "offs": striped(idx),
    }


def reference(query, kfirst, qrest, krest_words, krest_scales, size, vals, offs):
    idx = unstriped(offs)
    krestu = unpack_weight(krest_words, krest_scales, "e2m1")
    queryq = mxq(f64(query), 0, "e4m3")
    kfirstq = mxq(f64(kfirst), 0, "e4m3")
    a = queryq.T @ kfirstq
    qrestq = mxq(f64(qrest), 0, "e4m3")
    krestidxg = krestu[:, idx]
    b = qrestq.T @ krestidxg
    s = a[:, idx] + b
    p = np.exp(s - np.max(s, axis=1, keepdims=True))
    w = p * f64(size) / np.sum(p, axis=1, keepdims=True)
    wt = w.T
    vt = f64(vals)[:, idx].T
    vtq = mxq(vt, 0, "e4m3")
    wtq = mxq(wt, 0, "e4m3")
    o = vtq.T @ wtq
    words, scales = planes(o)
    return o, words, scales

@@ -1,0 +1,216 @@
+from contextlib import ExitStack
+
+import concourse.mybir as mybir
+from concourse.masks import make_identity
+
+D, T, I, Q, E, K = 512, 1024, 512, 256, 512, 1024
+FLOPS = 2 * Q * (D * T + K * I + I * E)
+
+F32 = mybir.dt.float32
+BF16 = mybir.dt.bfloat16
+I32 = mybir.dt.int32
+U32 = mybir.dt.uint32
+U16 = mybir.dt.uint16
+U8 = mybir.dt.uint8
+FP8X4 = mybir.dt.float8_e4m3fn_x4
+FP4X4 = mybir.dt.float4_e2m1fn_x4
+ALU = mybir.AluOpType
+ACT = mybir.ActivationFunctionType
+AX = mybir.AxisListType
+
+P = 128
+PACK = 4
+HALVES = Q // P
+CH = 256
+
+
+def tile_attend_prefixfeatures_pl_kernel(tc, query, kfirst, qrest, krest_words, krest_scales, size, vals, offs, out_0, out_1, out_2):
+    nc = tc.nc
+    with ExitStack() as ctx:
+        sb = ctx.enter_context(tc.tile_pool(name="sb", bufs=1))
+        ps = ctx.enter_context(tc.psum_pool(name="ps", bufs=1))
+
+        def tile(name, shape, dtype):
+            return sb.tile(shape, dtype, name=name, align_bytes=64)
+
+        def bank(name, tag, bufs, shape):
+            return ps.tile(shape, F32, name=name, tag=tag, bufs=bufs)
+
+        def weave(engine, name, raw):
+            width = raw.shape[2]
+            woven = tile(name, [P, width, PACK], BF16)
+            dst = woven[:].rearrange("p (c i) t -> p c t i", i=4)
+            src = raw.rearrange("p t (c i) -> p c t i", i=4)
+            if engine == "s":
+                nc.scalar.copy(out=dst, in_=src)
+            else:
+                nc.vector.tensor_copy(out=dst, in_=src)
+            return woven
+
+        def quantise(codes, scales, woven):
+            nc.vector.quantize_mx(out=codes.bitcast(FP8X4), scales=scales, in_=woven[:].rearrange("p w t -> p (w t)"))
+
+        offsets = sb.tile([P, I // 16], U16, name="offsets")
+        nc.sync.dma_start(offsets[:], offs)
+
+        sc_win = tile("sc_win", [P, T], U8)
+        nc.gpsimd.memset(sc_win[:].bitcast(I32), 0)
+        sc_hi = tile("sc_hi", [P, I], U8)
+        nc.gpsimd.memset(sc_hi[:].bitcast(I32), 0)
+        warm = tile("warm", [P, 1], F32)
+        nc.gpsimd.memset(warm[:], 0.0)
+        warm_out = tile("warm_out", [P, 1], F32)
+        nc.scalar.activation(out=warm_out[:], in_=warm[:], func=ACT.Exp)
+
+        ident = tile("ident", [P, P], F32)
+        make_identity(nc, ident[:])
+
+        w_win = []
+        for z in range(2):
+            win = tile("w_win%d" % z, [P, T], U16)
+            nc.sync.dma_start(out=win[:].bitcast(I32), in_=krest_words[z].bitcast(I32))
+            w_win.append(win)
+        for quad in range(4):
+            nc.sync.dma_start(
+                out=sc_win[32 * quad : 32 * quad + 8, :].bitcast(I32),
+                in_=krest_scales[:, 4 * quad : 4 * quad + 4, :].bitcast(I32),
+            )
+        q_raw = tile("q_raw", [P, PACK, Q], F32)
+        nc.sync.dma_start(out=q_raw[:], in_=query.rearrange("(p t) q -> p t q", t=PACK))
+        k_view = kfirst.rearrange("(p t) c -> p t c", t=PACK)
+        v_view = vals.rearrange("(p j) c -> p j c", j=PACK)
+        k_raw = [tile("k_raw%d" % th, [P, PACK, 512], F32) for th in range(2)]
+        v_win = [tile("v_win%d" % j, [P, T], F32) for j in range(PACK)]
+        r_raw = [tile("r_raw%d" % z, [P, PACK, Q], F32) for z in range(2)]
+        nc.sync.dma_start(out=k_raw[0][:], in_=k_view[:, :, 0:512])
+        size_col = tile("size_col", [P, PACK], F32)
+        nc.sync.dma_start(out=size_col[:], in_=size.rearrange("o (p r) -> p (o r)", r=PACK))
+        nc.sync.dma_start(out=v_win[0][:], in_=v_view[:, 0, :])
+        nc.sync.dma_start(out=k_raw[1][:], in_=k_view[:, :, 512:1024])
+        nc.sync.dma_start(out=v_win[1][:], in_=v_view[:, 1, :])
+        for z in range(2):
+            nc.sync.dma_start(out=r_raw[z][:], in_=qrest[512 * z : 512 * (z + 1), :].rearrange("(p t) q -> p t q", t=PACK))
+        nc.sync.dma_start(out=v_win[2][:], in_=v_view[:, 2, :])
+        nc.sync.dma_start(out=v_win[3][:], in_=v_view[:, 3, :])
+
+        w_got = []
+        for z in range(2):
+            got = tile("w_got%d" % z, [P, I], U16)
+            nc.vector.tensor_copy(got[:], w_win[z][:].indirect(offsets[:]))
+            w_got.append(got)
+        sc_got = tile("sc_got", [P, I], U8)
+        nc.vector.tensor_copy(sc_got[:], sc_win[:].indirect(offsets[:]))
+        nc.sync.dma_start(out=sc_hi[0:112, :].bitcast(I32), in_=sc_got[4:116, :].bitcast(I32))
+        sc_pass = [sc_got, sc_hi]
+
+        size_ps = bank("size_ps", "size", 1, [P, PACK, P])
+        for r in range(PACK):
+            nc.tensor.transpose(size_ps[:, r, :], size_col[:, r : r + 1].to_broadcast([P, P]), ident[:])
+
+        q_codes = tile("q_codes", [P, Q], U32)
+        q_scales = tile("q_scales", [P, Q], U8)
+        quantise(q_codes[:], q_scales[:], weave("s", "q_woven", q_raw[:]))
+
+        k_codes = tile("k_codes", [P, T], U32)
+        k_scales = tile("k_scales", [P, T], U8)
+        a_sb = [tile("a_sb%d" % h, [P, T], F32) for h in range(HALVES)]
+        vt_codes = tile("vt_codes", [P, E], U32)
+        vt_scales = tile("vt_scales", [P, E], U8)
+
+        def keys(th, engines):
+            woven = [weave(engines[c], "k_woven%d_%d" % (th, c), k_raw[th][:, :, CH * c : CH * (c + 1)]) for c in range(2)]
+            for c in range(2):
+                cols = slice(512 * th + CH * c, 512 * th + CH * (c + 1))
+                quantise(k_codes[:, cols], k_scales[:, cols], woven[c])
+            cols = slice(512 * th, 512 * (th + 1))
+            for h in range(HALVES):
+                rows = slice(P * h, P * (h + 1))
+                acc = bank("a_ps%d_%d" % (h, th), "mm", 3, [P, 512])
+                nc.tensor.matmul_mx(out=acc[:], lhsT=q_codes[:, rows].bitcast(FP8X4), lhsT_scale=q_scales[:, rows],
+                                    rhs=k_codes[:, cols].bitcast(FP8X4), rhs_scale=k_scales[:, cols], start=True, stop=True)
+                nc.scalar.copy(out=a_sb[h][:, cols], in_=acc[:])
+
+        def values(j):
+            got = tile("v_got%d" % j, [P, I], BF16)
+            nc.vector.tensor_copy(got[:], v_win[j][:].indirect(offsets[:]))
+            words = got[:].bitcast(F32)
+            turned = bank("v_ps%d" % j, "vt", 2, [P, 2, P])
+            for u in range(2):
+                nc.tensor.transpose(turned[:, u, :], words[:, u : I // 2 : 2], ident[:])
+            woven = tile("vt_woven%d" % j, [P, P, PACK], BF16)
+            nc.scalar.copy(out=woven[:].bitcast(F32), in_=turned[:].rearrange("p u e -> p e u"))
+            cols = slice(P * j, P * (j + 1))
+            quantise(vt_codes[:, cols], vt_scales[:, cols], woven)
+
+        keys(0, "sv")
+        values(0)
+        keys(1, "sv")
+        a_got = []
+        for h in range(HALVES):
+            got = tile("a_got%d" % h, [P, I], F32)
+            nc.vector.tensor_copy(got[:], a_sb[h][:].indirect(offsets[:]))
+            a_got.append(got)
+        values(1)
+
+        r_codes = [tile("r_codes%d" % z, [P, Q], U32) for z in range(2)]
+        r_scales = [tile("r_scales%d" % z, [P, Q], U8) for z in range(2)]
+        for z in range(2):
+            quantise(r_codes[z][:], r_scales[z][:], weave("s", "r_woven%d" % z, r_raw[z][:]))
+        b_ps = [bank("b_ps%d" % h, "b", 2, [P, I]) for h in range(HALVES)]
+        for z in range(2):
+            for h in range(HALVES):
+                rows = slice(P * h, P * (h + 1))
+                nc.tensor.matmul_mx(out=b_ps[h][:], lhsT=r_codes[z][:, rows].bitcast(FP8X4), lhsT_scale=r_scales[z][:, rows],
+                                    rhs=w_got[z][:].bitcast(FP4X4), rhs_scale=sc_pass[z][:], start=(z == 0), stop=(z == 1))
+        values(2)
+
+        wt_codes = tile("wt_codes", [P, Q], U32)
+        wt_scales = tile("wt_scales", [P, Q], U8)
+        p_sb, sums = [], []
+        for h in range(HALVES):
+            s = tile("s%d" % h, [P, I], F32)
+            nc.vector.tensor_tensor(s[:], b_ps[h][:], a_got[h][:], ALU.add)
+            neg_max = tile("neg_max%d" % h, [P, 1], F32)
+            nc.vector.tensor_reduce(neg_max[:], s[:], AX.X, ALU.max, negate=True)
+            p = tile("p%d" % h, [P, I], F32)
+            total = tile("total%d" % h, [P, 1], F32)
+            nc.scalar.activation(out=p[:], in_=s[:], func=ACT.Exp, bias=neg_max[:], scale=1.0, accum_out=total[:])
+            p_sb.append(p)
+            sums.append(total)
+        for h in range(HALVES):
+            rows = slice(P * h, P * (h + 1))
+            inv = tile("inv%d" % h, [P, 1], F32)
+            nc.vector.reciprocal(inv[:], sums[h][:])
+            w = tile("w%d" % h, [P, I], BF16)
+            nc.vector.scalar_tensor_tensor(
+                out=w[:].rearrange("p (s r) -> p s r", r=PACK), in0=p_sb[h][:].rearrange("p (s r) -> p s r", r=PACK),
+                scalar=inv[:], in1=size_ps[:].rearrange("p r s -> p s r"), op0=ALU.mult, op1=ALU.mult)
+            words = w[:].bitcast(F32)
+            turned = bank("w_ps%d" % h, "mm", 3, [P, 2, P])
+            for u in range(2):
+                nc.tensor.transpose(turned[:, u, :], words[:, u : I // 2 : 2], ident[:])
+            woven = tile("wt_woven%d" % h, [P, P, PACK], BF16)
+            nc.scalar.copy(out=woven[:].bitcast(F32), in_=turned[:].rearrange("p u q -> p q u"))
+            quantise(wt_codes[:, rows], wt_scales[:, rows], woven)
+            if h == 0:
+                values(3)
+
+        o_codes = tile("o_codes", [P, Q], U32)
+        o_scales = tile("o_scales", [P, Q], U8)
+        o_view = out_0.rearrange("(p j) q -> p j q", j=PACK)
+        for h in range(HALVES):
+            rows = slice(P * h, P * (h + 1))
+            acc = bank("o_ps%d" % h, "b", 2, [P, PACK, P])
+            for j in range(PACK):
+                cols = slice(P * j, P * (j + 1))
+                nc.tensor.matmul_mx(out=acc[:, j, :], lhsT=vt_codes[:, cols].bitcast(FP8X4), lhsT_scale=vt_scales[:, cols],
+                                    rhs=wt_codes[:, rows].bitcast(FP8X4), rhs_scale=wt_scales[:, rows], start=True, stop=True)
+            o_sb = tile("o_sb%d" % h, [P, PACK, P], F32)
+            nc.scalar.copy(out=o_sb[:], in_=acc[:])
+            nc.sync.dma_start(out=o_view[:, :, rows], in_=o_sb[:])
+            quantise(o_codes[:, rows], o_scales[:, rows], weave("v", "o_woven%d" % h, o_sb[:]))
+        nc.sync.dma_start(out=out_1[0].rearrange("p c r -> p (c r)").bitcast(I32), in_=o_codes[:].bitcast(I32))
+        for quad in range(4):
+            queue = nc.sync if quad % 2 == 0 else nc.scalar
+            queue.dma_start(out=out_2[0, 4 * quad : 4 * quad + 4, :].bitcast(I32),
+                            in_=o_scales[32 * quad : 32 * quad + 4, :].bitcast(I32))

@@ -22,6 +22,7 @@ P = 128
 PACK = 4
 HALVES = Q // P
 CH = 256
+K_LOADS = [(0, 512), (512, 1024)]
 
 
 def tile_attend_prefixfeatures_pl_kernel(tc, query, kfirst, qrest, krest_words, krest_scales, size, vals, offs, out_0, out_1, out_2):
@@ -30,8 +31,8 @@ def tile_attend_prefixfeatures_pl_kernel(tc, query, kfirst, qrest, krest_words, 
         sb = ctx.enter_context(tc.tile_pool(name="sb", bufs=1))
         ps = ctx.enter_context(tc.psum_pool(name="ps", bufs=1))
 
-        def tile(name, shape, dtype):
-            return sb.tile(shape, dtype, name=name, align_bytes=64)
+        def tile(name, shape, dtype, slot=None):
+            return sb.tile(shape, dtype, name=name, tag=slot or name, align_bytes=64)
 
         def bank(name, tag, bufs, shape):
             return ps.tile(shape, F32, name=name, tag=tag, bufs=bufs)
@@ -53,10 +54,8 @@ def tile_attend_prefixfeatures_pl_kernel(tc, query, kfirst, qrest, krest_words, 
         offsets = sb.tile([P, I // 16], U16, name="offsets")
         nc.sync.dma_start(offsets[:], offs)
 
-        sc_win = tile("sc_win", [P, T], U8)
+        sc_win = tile("sc_win", [P, 2 * T], U8)
         nc.gpsimd.memset(sc_win[:].bitcast(I32), 0)
-        sc_hi = tile("sc_hi", [P, I], U8)
-        nc.gpsimd.memset(sc_hi[:].bitcast(I32), 0)
         warm = tile("warm", [P, 1], F32)
         nc.gpsimd.memset(warm[:], 0.0)
         warm_out = tile("warm_out", [P, 1], F32)
@@ -72,36 +71,33 @@ def tile_attend_prefixfeatures_pl_kernel(tc, query, kfirst, qrest, krest_words, 
             w_win.append(win)
         for quad in range(4):
             nc.sync.dma_start(
-                out=sc_win[32 * quad : 32 * quad + 8, :].bitcast(I32),
-                in_=krest_scales[:, 4 * quad : 4 * quad + 4, :].bitcast(I32),
+                out=sc_win[32 * quad : 32 * quad + 4, :].bitcast(I32).rearrange("r (z c) -> r z c", z=2),
+                in_=krest_scales[:, 4 * quad : 4 * quad + 4, :].bitcast(I32).rearrange("z r c -> r z c"),
             )
         q_raw = tile("q_raw", [P, PACK, Q], F32)
         nc.sync.dma_start(out=q_raw[:], in_=query.rearrange("(p t) q -> p t q", t=PACK))
         k_view = kfirst.rearrange("(p t) c -> p t c", t=PACK)
         v_view = vals.rearrange("(p j) c -> p j c", j=PACK)
-        k_raw = [tile("k_raw%d" % th, [P, PACK, 512], F32) for th in range(2)]
+        k_raw = [tile("k_raw%d" % c, [P, PACK, hi - lo], F32) for c, (lo, hi) in enumerate(K_LOADS)]
         v_win = [tile("v_win%d" % j, [P, T], F32) for j in range(PACK)]
         r_raw = [tile("r_raw%d" % z, [P, PACK, Q], F32) for z in range(2)]
-        nc.sync.dma_start(out=k_raw[0][:], in_=k_view[:, :, 0:512])
-        size_col = tile("size_col", [P, PACK], F32)
-        nc.sync.dma_start(out=size_col[:], in_=size.rearrange("o (p r) -> p (o r)", r=PACK))
-        nc.sync.dma_start(out=v_win[0][:], in_=v_view[:, 0, :])
-        nc.sync.dma_start(out=k_raw[1][:], in_=k_view[:, :, 512:1024])
-        nc.sync.dma_start(out=v_win[1][:], in_=v_view[:, 1, :])
         for z in range(2):
             nc.sync.dma_start(out=r_raw[z][:], in_=qrest[512 * z : 512 * (z + 1), :].rearrange("(p t) q -> p t q", t=PACK))
-        nc.sync.dma_start(out=v_win[2][:], in_=v_view[:, 2, :])
-        nc.sync.dma_start(out=v_win[3][:], in_=v_view[:, 3, :])
+        size_col = tile("size_col", [P, PACK], F32)
+        nc.sync.dma_start(out=size_col[:], in_=size.rearrange("o (p r) -> p (o r)", r=PACK))
+        for c, (lo, hi) in enumerate(K_LOADS):
+            nc.sync.dma_start(out=k_raw[c][:], in_=k_view[:, :, lo:hi])
+        for j in range(PACK):
+            nc.sync.dma_start(out=v_win[j][:], in_=v_view[:, j, :])
 
-        w_got = []
+        w_got, sc_pass = [], []
         for z in range(2):
             got = tile("w_got%d" % z, [P, I], U16)
             nc.vector.tensor_copy(got[:], w_win[z][:].indirect(offsets[:]))
             w_got.append(got)
-        sc_got = tile("sc_got", [P, I], U8)
-        nc.vector.tensor_copy(sc_got[:], sc_win[:].indirect(offsets[:]))
-        nc.sync.dma_start(out=sc_hi[0:112, :].bitcast(I32), in_=sc_got[4:116, :].bitcast(I32))
-        sc_pass = [sc_got, sc_hi]
+            sc_got = tile("sc_got%d" % z, [P, I], U8)
+            nc.vector.tensor_copy(sc_got[:], sc_win[:, T * z : T * (z + 1)].indirect(offsets[:]))
+            sc_pass.append(sc_got)
 
         size_ps = bank("size_ps", "size", 1, [P, PACK, P])
         for r in range(PACK):
@@ -117,22 +113,31 @@ def tile_attend_prefixfeatures_pl_kernel(tc, query, kfirst, qrest, krest_words, 
         vt_codes = tile("vt_codes", [P, E], U32)
         vt_scales = tile("vt_scales", [P, E], U8)
 
-        def keys(th, engines):
-            woven = [weave(engines[c], "k_woven%d_%d" % (th, c), k_raw[th][:, :, CH * c : CH * (c + 1)]) for c in range(2)]
-            for c in range(2):
-                cols = slice(512 * th + CH * c, 512 * th + CH * (c + 1))
-                quantise(k_codes[:, cols], k_scales[:, cols], woven[c])
-            cols = slice(512 * th, 512 * (th + 1))
+        def keys(c, engines):
+            lo, hi = K_LOADS[c]
+            woven = [weave(e, "k_woven%d_%d" % (c, n), k_raw[c][:, :, CH * n : CH * (n + 1)]) for n, e in enumerate(engines)]
+            for n in range(len(engines)):
+                cols = slice(lo + CH * n, lo + CH * (n + 1))
+                quantise(k_codes[:, cols], k_scales[:, cols], woven[n])
+            cols = slice(lo, hi)
             for h in range(HALVES):
                 rows = slice(P * h, P * (h + 1))
-                acc = bank("a_ps%d_%d" % (h, th), "mm", 3, [P, 512])
+                acc = bank("a_ps%d_%d" % (h, c), "mm", 3, [P, hi - lo])
                 nc.tensor.matmul_mx(out=acc[:], lhsT=q_codes[:, rows].bitcast(FP8X4), lhsT_scale=q_scales[:, rows],
                                     rhs=k_codes[:, cols].bitcast(FP8X4), rhs_scale=k_scales[:, cols], start=True, stop=True)
                 nc.scalar.copy(out=a_sb[h][:, cols], in_=acc[:])
 
-        def values(j):
-            got = tile("v_got%d" % j, [P, I], BF16)
-            nc.vector.tensor_copy(got[:], v_win[j][:].indirect(offsets[:]))
+        def values(j, engine, got_slot=None, rounded_slot=None):
+            got = tile("v_got%d" % j, [P, I], BF16, got_slot)
+            if engine != "v":
+                rounded = tile("v_rounded%d" % j, [P, T], BF16, rounded_slot)
+                if engine == "ss":
+                    nc.scalar.activation(out=rounded[:], in_=v_win[j][:], func=ACT.Copy)
+                else:
+                    nc.vector.tensor_copy(rounded[:], v_win[j][:])
+                nc.scalar.activation(out=got[:], in_=rounded[:].indirect(offsets[:]), func=ACT.Copy)
+            else:
+                nc.vector.tensor_copy(got[:], v_win[j][:].indirect(offsets[:]))
             words = got[:].bitcast(F32)
             turned = bank("v_ps%d" % j, "vt", 2, [P, 2, P])
             for u in range(2):
@@ -141,16 +146,6 @@ def tile_attend_prefixfeatures_pl_kernel(tc, query, kfirst, qrest, krest_words, 
             nc.scalar.copy(out=woven[:].bitcast(F32), in_=turned[:].rearrange("p u e -> p e u"))
             cols = slice(P * j, P * (j + 1))
             quantise(vt_codes[:, cols], vt_scales[:, cols], woven)
-
-        keys(0, "sv")
-        values(0)
-        keys(1, "sv")
-        a_got = []
-        for h in range(HALVES):
-            got = tile("a_got%d" % h, [P, I], F32)
-            nc.vector.tensor_copy(got[:], a_sb[h][:].indirect(offsets[:]))
-            a_got.append(got)
-        values(1)
 
         r_codes = [tile("r_codes%d" % z, [P, Q], U32) for z in range(2)]
         r_scales = [tile("r_scales%d" % z, [P, Q], U8) for z in range(2)]
@@ -162,14 +157,18 @@ def tile_attend_prefixfeatures_pl_kernel(tc, query, kfirst, qrest, krest_words, 
                 rows = slice(P * h, P * (h + 1))
                 nc.tensor.matmul_mx(out=b_ps[h][:], lhsT=r_codes[z][:, rows].bitcast(FP8X4), lhsT_scale=r_scales[z][:, rows],
                                     rhs=w_got[z][:].bitcast(FP4X4), rhs_scale=sc_pass[z][:], start=(z == 0), stop=(z == 1))
-        values(2)
+        keys(0, "sv")
+        b_sb = tile("b_sb", [P, HALVES, I], F32, "k_raw0")
+        for h in range(HALVES):
+            nc.scalar.copy(out=b_sb[:, h, :], in_=b_ps[h][:])
+        keys(1, "vv")
 
         wt_codes = tile("wt_codes", [P, Q], U32)
         wt_scales = tile("wt_scales", [P, Q], U8)
         p_sb, sums = [], []
         for h in range(HALVES):
             s = tile("s%d" % h, [P, I], F32)
-            nc.vector.tensor_tensor(s[:], b_ps[h][:], a_got[h][:], ALU.add)
+            nc.vector.tensor_tensor(s[:], a_sb[h][:].indirect(offsets[:]), b_sb[:, h, :], ALU.add)
             neg_max = tile("neg_max%d" % h, [P, 1], F32)
             nc.vector.tensor_reduce(neg_max[:], s[:], AX.X, ALU.max, negate=True)
             p = tile("p%d" % h, [P, I], F32)
@@ -192,8 +191,10 @@ def tile_attend_prefixfeatures_pl_kernel(tc, query, kfirst, qrest, krest_words, 
             woven = tile("wt_woven%d" % h, [P, P, PACK], BF16)
             nc.scalar.copy(out=woven[:].bitcast(F32), in_=turned[:].rearrange("p u q -> p q u"))
             quantise(wt_codes[:, rows], wt_scales[:, rows], woven)
-            if h == 0:
-                values(3)
+        values(0, "ss")
+        values(1, "v")
+        values(2, "ss")
+        values(3, "v")
 
         o_codes = tile("o_codes", [P, Q], U32)
         o_scales = tile("o_scales", [P, Q], U8)

from contextlib import ExitStack

import concourse.mybir as mybir
from concourse.masks import make_identity

D, T, I, Q, E, K = 512, 1024, 512, 256, 512, 1024
FLOPS = 2 * Q * (D * T + K * I + I * E)

F32 = mybir.dt.float32
BF16 = mybir.dt.bfloat16
I32 = mybir.dt.int32
U32 = mybir.dt.uint32
U16 = mybir.dt.uint16
U8 = mybir.dt.uint8
FP8X4 = mybir.dt.float8_e4m3fn_x4
FP4X4 = mybir.dt.float4_e2m1fn_x4
ALU = mybir.AluOpType
ACT = mybir.ActivationFunctionType
AX = mybir.AxisListType

P = 128
PACK = 4
HALVES = Q // P
CH = 256
K_LOADS = [(0, 512), (512, 1024)]


def tile_attend_prefixfeatures_pl_kernel(tc, query, kfirst, qrest, krest_words, krest_scales, size, vals, offs, out_0, out_1, out_2):
    nc = tc.nc
    with ExitStack() as ctx:
        sb = ctx.enter_context(tc.tile_pool(name="sb", bufs=1))
        ps = ctx.enter_context(tc.psum_pool(name="ps", bufs=1))

        def tile(name, shape, dtype, slot=None):
            return sb.tile(shape, dtype, name=name, tag=slot or name, align_bytes=64)

        def bank(name, tag, bufs, shape):
            return ps.tile(shape, F32, name=name, tag=tag, bufs=bufs)

        def weave(engine, name, raw):
            width = raw.shape[2]
            woven = tile(name, [P, width, PACK], BF16)
            dst = woven[:].rearrange("p (c i) t -> p c t i", i=4)
            src = raw.rearrange("p t (c i) -> p c t i", i=4)
            if engine == "s":
                nc.scalar.copy(out=dst, in_=src)
            else:
                nc.vector.tensor_copy(out=dst, in_=src)
            return woven

        def quantise(codes, scales, woven):
            nc.vector.quantize_mx(out=codes.bitcast(FP8X4), scales=scales, in_=woven[:].rearrange("p w t -> p (w t)"))

        offsets = sb.tile([P, I // 16], U16, name="offsets")
        nc.sync.dma_start(offsets[:], offs)

        sc_win = tile("sc_win", [P, 2 * T], U8)
        nc.gpsimd.memset(sc_win[:].bitcast(I32), 0)
        warm = tile("warm", [P, 1], F32)
        nc.gpsimd.memset(warm[:], 0.0)
        warm_out = tile("warm_out", [P, 1], F32)
        nc.scalar.activation(out=warm_out[:], in_=warm[:], func=ACT.Exp)

        ident = tile("ident", [P, P], F32)
        make_identity(nc, ident[:])

        w_win = []
        for z in range(2):
            win = tile("w_win%d" % z, [P, T], U16)
            nc.sync.dma_start(out=win[:].bitcast(I32), in_=krest_words[z].bitcast(I32))
            w_win.append(win)
        for quad in range(4):
            nc.sync.dma_start(
                out=sc_win[32 * quad : 32 * quad + 4, :].bitcast(I32).rearrange("r (z c) -> r z c", z=2),
                in_=krest_scales[:, 4 * quad : 4 * quad + 4, :].bitcast(I32).rearrange("z r c -> r z c"),
            )
        q_raw = tile("q_raw", [P, PACK, Q], F32)
        nc.sync.dma_start(out=q_raw[:], in_=query.rearrange("(p t) q -> p t q", t=PACK))
        k_view = kfirst.rearrange("(p t) c -> p t c", t=PACK)
        v_view = vals.rearrange("(p j) c -> p j c", j=PACK)
        k_raw = [tile("k_raw%d" % c, [P, PACK, hi - lo], F32) for c, (lo, hi) in enumerate(K_LOADS)]
        v_win = [tile("v_win%d" % j, [P, T], F32) for j in range(PACK)]
        r_raw = [tile("r_raw%d" % z, [P, PACK, Q], F32) for z in range(2)]
        for z in range(2):
            nc.sync.dma_start(out=r_raw[z][:], in_=qrest[512 * z : 512 * (z + 1), :].rearrange("(p t) q -> p t q", t=PACK))
        size_col = tile("size_col", [P, PACK], F32)
        nc.sync.dma_start(out=size_col[:], in_=size.rearrange("o (p r) -> p (o r)", r=PACK))
        for c, (lo, hi) in enumerate(K_LOADS):
            nc.sync.dma_start(out=k_raw[c][:], in_=k_view[:, :, lo:hi])
        for j in range(PACK):
            nc.sync.dma_start(out=v_win[j][:], in_=v_view[:, j, :])

        w_got, sc_pass = [], []
        for z in range(2):
            got = tile("w_got%d" % z, [P, I], U16)
            nc.vector.tensor_copy(got[:], w_win[z][:].indirect(offsets[:]))
            w_got.append(got)
            sc_got = tile("sc_got%d" % z, [P, I], U8)
            nc.vector.tensor_copy(sc_got[:], sc_win[:, T * z : T * (z + 1)].indirect(offsets[:]))
            sc_pass.append(sc_got)

        size_ps = bank("size_ps", "size", 1, [P, PACK, P])
        for r in range(PACK):
            nc.tensor.transpose(size_ps[:, r, :], size_col[:, r : r + 1].to_broadcast([P, P]), ident[:])

        q_codes = tile("q_codes", [P, Q], U32)
        q_scales = tile("q_scales", [P, Q], U8)
        quantise(q_codes[:], q_scales[:], weave("s", "q_woven", q_raw[:]))

        k_codes = tile("k_codes", [P, T], U32)
        k_scales = tile("k_scales", [P, T], U8)
        a_sb = [tile("a_sb%d" % h, [P, T], F32) for h in range(HALVES)]
        vt_codes = tile("vt_codes", [P, E], U32)
        vt_scales = tile("vt_scales", [P, E], U8)

        def keys(c, engines):
            lo, hi = K_LOADS[c]
            woven = [weave(e, "k_woven%d_%d" % (c, n), k_raw[c][:, :, CH * n : CH * (n + 1)]) for n, e in enumerate(engines)]
            for n in range(len(engines)):
                cols = slice(lo + CH * n, lo + CH * (n + 1))
                quantise(k_codes[:, cols], k_scales[:, cols], woven[n])
            cols = slice(lo, hi)
            for h in range(HALVES):
                rows = slice(P * h, P * (h + 1))
                acc = bank("a_ps%d_%d" % (h, c), "mm", 3, [P, hi - lo])
                nc.tensor.matmul_mx(out=acc[:], lhsT=q_codes[:, rows].bitcast(FP8X4), lhsT_scale=q_scales[:, rows],
                                    rhs=k_codes[:, cols].bitcast(FP8X4), rhs_scale=k_scales[:, cols], start=True, stop=True)
                nc.scalar.copy(out=a_sb[h][:, cols], in_=acc[:])

        def values(j, engine, got_slot=None, rounded_slot=None):
            got = tile("v_got%d" % j, [P, I], BF16, got_slot)
            if engine != "v":
                rounded = tile("v_rounded%d" % j, [P, T], BF16, rounded_slot)
                if engine == "ss":
                    nc.scalar.activation(out=rounded[:], in_=v_win[j][:], func=ACT.Copy)
                else:
                    nc.vector.tensor_copy(rounded[:], v_win[j][:])
                nc.scalar.activation(out=got[:], in_=rounded[:].indirect(offsets[:]), func=ACT.Copy)
            else:
                nc.vector.tensor_copy(got[:], v_win[j][:].indirect(offsets[:]))
            words = got[:].bitcast(F32)
            turned = bank("v_ps%d" % j, "vt", 2, [P, 2, P])
            for u in range(2):
                nc.tensor.transpose(turned[:, u, :], words[:, u : I // 2 : 2], ident[:])
            woven = tile("vt_woven%d" % j, [P, P, PACK], BF16)
            nc.scalar.copy(out=woven[:].bitcast(F32), in_=turned[:].rearrange("p u e -> p e u"))
            cols = slice(P * j, P * (j + 1))
            quantise(vt_codes[:, cols], vt_scales[:, cols], woven)

        r_codes = [tile("r_codes%d" % z, [P, Q], U32) for z in range(2)]
        r_scales = [tile("r_scales%d" % z, [P, Q], U8) for z in range(2)]
        for z in range(2):
            quantise(r_codes[z][:], r_scales[z][:], weave("s", "r_woven%d" % z, r_raw[z][:]))
        b_ps = [bank("b_ps%d" % h, "b", 2, [P, I]) for h in range(HALVES)]
        for z in range(2):
            for h in range(HALVES):
                rows = slice(P * h, P * (h + 1))
                nc.tensor.matmul_mx(out=b_ps[h][:], lhsT=r_codes[z][:, rows].bitcast(FP8X4), lhsT_scale=r_scales[z][:, rows],
                                    rhs=w_got[z][:].bitcast(FP4X4), rhs_scale=sc_pass[z][:], start=(z == 0), stop=(z == 1))
        keys(0, "sv")
        b_sb = tile("b_sb", [P, HALVES, I], F32, "k_raw0")
        for h in range(HALVES):
            nc.scalar.copy(out=b_sb[:, h, :], in_=b_ps[h][:])
        keys(1, "vv")

        wt_codes = tile("wt_codes", [P, Q], U32)
        wt_scales = tile("wt_scales", [P, Q], U8)
        p_sb, sums = [], []
        for h in range(HALVES):
            s = tile("s%d" % h, [P, I], F32)
            nc.vector.tensor_tensor(s[:], a_sb[h][:].indirect(offsets[:]), b_sb[:, h, :], ALU.add)
            neg_max = tile("neg_max%d" % h, [P, 1], F32)
            nc.vector.tensor_reduce(neg_max[:], s[:], AX.X, ALU.max, negate=True)
            p = tile("p%d" % h, [P, I], F32)
            total = tile("total%d" % h, [P, 1], F32)
            nc.scalar.activation(out=p[:], in_=s[:], func=ACT.Exp, bias=neg_max[:], scale=1.0, accum_out=total[:])
            p_sb.append(p)
            sums.append(total)
        for h in range(HALVES):
            rows = slice(P * h, P * (h + 1))
            inv = tile("inv%d" % h, [P, 1], F32)
            nc.vector.reciprocal(inv[:], sums[h][:])
            w = tile("w%d" % h, [P, I], BF16)
            nc.vector.scalar_tensor_tensor(
                out=w[:].rearrange("p (s r) -> p s r", r=PACK), in0=p_sb[h][:].rearrange("p (s r) -> p s r", r=PACK),
                scalar=inv[:], in1=size_ps[:].rearrange("p r s -> p s r"), op0=ALU.mult, op1=ALU.mult)
            words = w[:].bitcast(F32)
            turned = bank("w_ps%d" % h, "mm", 3, [P, 2, P])
            for u in range(2):
                nc.tensor.transpose(turned[:, u, :], words[:, u : I // 2 : 2], ident[:])
            woven = tile("wt_woven%d" % h, [P, P, PACK], BF16)
            nc.scalar.copy(out=woven[:].bitcast(F32), in_=turned[:].rearrange("p u q -> p q u"))
            quantise(wt_codes[:, rows], wt_scales[:, rows], woven)
        values(0, "ss")
        values(1, "v")
        values(2, "ss")
        values(3, "v")

        o_codes = tile("o_codes", [P, Q], U32)
        o_scales = tile("o_scales", [P, Q], U8)
        o_view = out_0.rearrange("(p j) q -> p j q", j=PACK)
        for h in range(HALVES):
            rows = slice(P * h, P * (h + 1))
            acc = bank("o_ps%d" % h, "b", 2, [P, PACK, P])
            for j in range(PACK):
                cols = slice(P * j, P * (j + 1))
                nc.tensor.matmul_mx(out=acc[:, j, :], lhsT=vt_codes[:, cols].bitcast(FP8X4), lhsT_scale=vt_scales[:, cols],
                                    rhs=wt_codes[:, rows].bitcast(FP8X4), rhs_scale=wt_scales[:, rows], start=True, stop=True)
            o_sb = tile("o_sb%d" % h, [P, PACK, P], F32)
            nc.scalar.copy(out=o_sb[:], in_=acc[:])
            nc.sync.dma_start(out=o_view[:, :, rows], in_=o_sb[:])
            quantise(o_codes[:, rows], o_scales[:, rows], weave("v", "o_woven%d" % h, o_sb[:]))
        nc.sync.dma_start(out=out_1[0].rearrange("p c r -> p (c r)").bitcast(I32), in_=o_codes[:].bitcast(I32))
        for quad in range(4):
            queue = nc.sync if quad % 2 == 0 else nc.scalar
            queue.dma_start(out=out_2[0, 4 * quad : 4 * quad + 4, :].bitcast(I32),
                            in_=o_scales[32 * quad : 32 * quad + 4, :].bitcast(I32))
